import numpy as np
import ml_dtypes


def mxq(x, axis, fmt="e4m3"):
    dtype, down = {"e4m3": (ml_dtypes.float8_e4m3fn, 7), "e5m2": (ml_dtypes.float8_e5m2, 14)}[fmt]
    v = np.moveaxis(np.asarray(x, np.float32).astype(ml_dtypes.bfloat16).astype(np.float64), axis, -1)
    blocks = v.reshape(v.shape[:-1] + (-1, 32))
    amax = np.abs(blocks).max(-1, keepdims=True)
    byte = np.maximum(np.where(amax > 0, np.frexp(amax)[1] - 1 + 127, 0) - down, 1)
    scale = np.exp2(byte - 127.0)
    codes = (blocks / scale).astype(np.float32).astype(dtype).astype(np.float64)
    return np.moveaxis((codes * scale).reshape(v.shape), -1, axis)


WIDE = False


def mx_kscale(k):
    if not WIDE:
        return np.ones(k)
    levels = np.array([10, -10, 5, -5, 0])
    if k % 512:
        return np.exp2(np.random.permutation(np.resize(levels, k // 32))).repeat(32)
    a = np.empty((k // 512, 16))
    for p in range(k // 512):
        a[p, :8] = np.random.permutation(np.resize(levels, 8))
        for g in range(8):
            far = levels[np.abs(levels - a[p, g]) >= 10]
            a[p, g + 8] = far[np.random.randint(len(far))]
    return np.exp2(a.ravel()).repeat(32)


def f64(x):
    return np.asarray(x).astype(np.float64)


def striped(idx):
    return np.tile(idx.reshape(-1, 16).T, (8, 1)).astype(np.uint16)


def unstriped(offs):
    return offs[:16].T.reshape(-1).astype(np.int64)


def striped8(idx):
    return np.concatenate([x.reshape(-1, 16).T for x in idx]).astype(np.uint16)


def runs(offs, k):
    lists = np.stack([offs[16 * r : 16 * r + 16].T.reshape(-1) for r in range(8)]).astype(np.int64)
    return lists[np.arange(k) % 512 // 64]


def pack_weight(w):
    k, n = w.shape
    w = f64(np.asarray(w, np.float32).astype(ml_dtypes.bfloat16)).reshape(k // 32, 32, n)
    amax = np.abs(w).max(1)
    byte = np.clip(np.where(amax > 0, np.frexp(amax)[1] - 1 + 127 - 7, 1), 1, 254)
    scaled = (w * np.exp2(127.0 - byte)[:, None, :]).reshape(k, n).astype(np.float32)
    words = np.ascontiguousarray(scaled.reshape(k // 512, 128, 4, n).transpose(0, 1, 3, 2)).astype(ml_dtypes.float8_e4m3fn).view(np.uint8)
    return words, np.ascontiguousarray(byte.astype(np.uint8).reshape(k // 512, 16, n))


def unpack_weight(words, scales):
    g, p, n, _ = words.shape
    vals = np.ascontiguousarray(words).view(ml_dtypes.float8_e4m3fn).astype(np.float64) * np.repeat(np.exp2(scales.astype(np.float64) - 127.0), 8, axis=1)[..., None]
    return vals.transpose(0, 1, 3, 2).reshape(g * 512, n)


def sigmoid(v):
    return 1.0 / (1.0 + np.exp(-np.maximum(v, -700.0)))

def planes(y):
    n, m = y.shape
    v = y.astype(np.float32).astype(ml_dtypes.bfloat16).astype(np.float64).reshape(n // 32, 32, m)
    top = np.abs(v).max(1)
    byte = np.clip(np.where(top > 0, np.frexp(top)[1] - 1 + 127 - 7, 1), 1, 254)
    codes = (v * np.exp2(127.0 - byte)[:, None, :]).reshape(n, m).astype(np.float32).astype(ml_dtypes.float8_e4m3fn).view(np.uint8)
    words = codes.reshape(n // 512, 128, 4, m).transpose(0, 1, 3, 2)
    return np.ascontiguousarray(words), np.ascontiguousarray(byte.astype(np.uint8).reshape(n // 512, 16, m))


K, T, S, H, C = 512, 2048, 512, 512, 512


def setup_inputs():
    n = np.random.standard_normal
    s = mx_kscale(K)[:, None]
    packed_xT = pack_weight(n((K, T)) * s)
    packed_w1 = pack_weight(n((K, H)) / np.sqrt(K) / s)
    return {
        "x_words": packed_xT[0],
        "x_scales": packed_xT[1],
        "w1_words": packed_w1[0],
        "w1_scales": packed_w1[1],
        "gs": (np.random.uniform(0.5, 1.5, (K, 1)) / s).astype(np.float32),
        "offs": striped(np.random.permutation(T)[:S]),
        "n1": striped8(np.stack([np.random.permutation(S) for _ in range(8)])),
        "n2": striped8(np.stack([np.random.permutation(S) for _ in range(8)])),
        "ca": striped(np.random.permutation(T)[:C]),
        "cb": striped(np.random.permutation(T)[:C]),
        "n3": striped8(np.stack([np.random.permutation(S) for _ in range(8)])),
        "n4": striped8(np.stack([np.random.permutation(S) for _ in range(8)])),
        "n5": striped8(np.stack([np.random.permutation(S) for _ in range(8)])),
    }


def reference(x_words, x_scales, w1_words, w1_scales, gs, offs, n1, n2, ca, cb, n3, n4, n5):
    x_ca = unpack_weight(x_words, x_scales)[:, unstriped(ca)]
    xq = unpack_weight(x_words, x_scales)[:, unstriped(offs)]
    y = unpack_weight(w1_words, w1_scales).T @ xq
    z = f64(gs) * (np.maximum(y * (sigmoid(y[np.arange(H)[:, None], runs(n1, H)])), y[np.arange(H)[:, None], runs(n2, H)]))
    zq = mxq(z, 0, "e4m3")
    a = 0.0625 * (x_ca.T @ zq)
    x_cb = unpack_weight(x_words, x_scales)[:, unstriped(cb)]
    b = 0.0625 * (x_cb.T @ zq)
    out_0 = np.maximum(np.minimum(a - (0.5 * (a[np.arange(C)[:, None], runs(n3, C)])), b[np.arange(C)[:, None], runs(n4, C)]), b[np.arange(C)[:, None], runs(n5, C)])
    return (out_0,) + planes(out_0)

@@ -1,0 +1,221 @@
+from contextlib import ExitStack
+
+import concourse.mybir as mybir
+
+F32 = mybir.dt.float32
+BF16 = mybir.dt.bfloat16
+I32 = mybir.dt.int32
+U32 = mybir.dt.uint32
+U16 = mybir.dt.uint16
+U8 = mybir.dt.uint8
+FP8X4 = mybir.dt.float8_e4m3fn_x4
+ALU = mybir.AluOpType
+ACT = mybir.ActivationFunctionType
+
+P = 128
+PACK = 4
+T = 2048
+S = 512
+HALF = S // 2
+FLOPS = 3 * 2 * 512 * 512 * 512
+OUT_CHUNKS = ((0, 256), (256, 384), (384, 512))
+
+
+def tile_picked_ccmpclampbgmax_none_po_kernel(tc, x_words, x_scales, w1_words, w1_scales, gs, offs, n1, n2, ca, cb, n3, n4, n5, out_0, out_1, out_2):
+    nc = tc.nc
+    with ExitStack() as ctx:
+        keep = ctx.enter_context(tc.tile_pool(name="keep", bufs=1))
+        psum = ctx.enter_context(tc.psum_pool(name="psum", bufs=1))
+
+        def new(name, shape, dtype):
+            return keep.tile(shape, dtype, name=name, align_bytes=64)
+
+        def load_list(name, src):
+            tile = keep.tile([P, S // 16], U16, name=name)
+            nc.sync.dma_start(tile[:], src)
+            return tile
+
+        def load_scales(tile, src):
+            for q in range(4):
+                nc.sync.dma_start(tile[32 * q : 32 * q + 4, :].bitcast(I32), src[0, 4 * q : 4 * q + 4, :].bitcast(I32))
+
+        def load_words(tile, src):
+            nc.sync.dma_start(tile[:].bitcast(I32), src[0].rearrange("p n t -> p (n t)").bitcast(I32))
+
+        def deal(engine, dst, src, run):
+            engine.tensor_copy(
+                dst[:].rearrange("p (t c i) -> p c t i", t=PACK, i=run),
+                src[:].rearrange("p (c i t) -> p c t i", t=PACK, i=run),
+            )
+
+        def entries(tile, lo, hi):
+            return tile[:, lo // 16 : hi // 16]
+
+        def interleave(copy, dst, src):
+            copy(dst[:].rearrange("p (c i t) -> p c t i", t=PACK, i=4), src[:].rearrange("p t (c i) -> p c t i", i=4))
+
+        xs = new("xs", [P, T], U8)
+        ws = new("ws", [P, S], U8)
+        nc.vector.memset(xs[:].bitcast(I32), 0)
+        nc.gpsimd.memset(ws[:].bitcast(I32), 0)
+        warm = new("warm", [P, 1], F32)
+        warm_out = new("warm_out", [P, 1], F32)
+        nc.gpsimd.memset(warm[:], 0.0)
+        nc.scalar.activation(warm_out[:], warm[:], ACT.Sigmoid)
+
+        offs_t = load_list("offs_t", offs)
+        ca_t = load_list("ca_t", ca)
+        cb_t = load_list("cb_t", cb)
+        load_scales(xs, x_scales)
+        xw = new("xw", [P, T], U32)
+        load_words(xw, x_words)
+        ww = new("ww", [P, S], U32)
+        load_words(ww, w1_words)
+        load_scales(ws, w1_scales)
+        n1_t = load_list("n1_t", n1)
+        n2_t = load_list("n2_t", n2)
+        gs_t = new("gs_t", [P, PACK], F32)
+        nc.sync.dma_start(gs_t[:], gs.rearrange("(p t) o -> p (t o)", t=PACK))
+        n3_t = load_list("n3_t", n3)
+        n4_t = load_list("n4_t", n4)
+        n5_t = load_list("n5_t", n5)
+
+        ww_d = new("ww_d", [P, S], U32)
+        ws_d = new("ws_d", [P, S], U8)
+        deal(nc.gpsimd, ww_d, ww, 4)
+        deal(nc.gpsimd, ws_d, ws, 16)
+
+        def pick(name, table, dtype, lst):
+            tile = new(name, [P, S], dtype)
+            nc.vector.tensor_copy(tile[:], table[:].indirect(lst[:]))
+            return tile
+
+        def dealt(name, tile, dtype, run):
+            res = new(name, [P, S], dtype)
+            deal(nc.vector, res, tile, run)
+            return res
+
+        xq_s = pick("xq_s", xs, U8, offs_t)
+        ca_s = pick("ca_s", xs, U8, ca_t)
+        cb_s = pick("cb_s", xs, U8, cb_t)
+        xq_w = pick("xq_w", xw, U32, offs_t)
+        ca_w = pick("ca_w", xw, U32, ca_t)
+        ca_wd = dealt("ca_wd", ca_w, U32, 4)
+        ca_sd = dealt("ca_sd", ca_s, U8, 16)
+
+        def product(dst, lw, ls, t, rw, rs):
+            cols = slice(P * t, P * (t + 1))
+            nc.tensor.matmul_mx(out=dst, lhsT=lw[:, cols].bitcast(FP8X4), lhsT_scale=ls[:, cols],
+                                rhs=rw.bitcast(FP8X4), rhs_scale=rs, start=True, stop=True)
+
+        y = [new(f"y{t}", [P, S], F32) for t in range(PACK)]
+        sig = [new(f"sig{h}", [P, PACK, HALF], F32) for h in range(2)]
+        got = [new(f"got{h}", [P, PACK, HALF], F32) for h in range(2)]
+        gated = [new(f"gated{h}", [P, PACK, HALF], F32) for h in range(2)]
+        larger = [new(f"larger{h}", [P, PACK, HALF], F32) for h in range(2)]
+        zp = [new(f"zp{h}", [P, PACK, HALF], BF16) for h in range(2)]
+        zi = [new(f"zi{h}", [P, PACK * HALF], BF16) for h in range(2)]
+        zw = new("zw", [P, S], U32)
+        zs = new("zs", [P, S], U8)
+        a_ps = [psum.tile([P, S], F32, name=f"a_ps{t}") for t in range(PACK)]
+        a_half = [new(f"a_half{t}", [P, S], F32) for t in range(PACK)]
+        a_full = [new(f"a_full{t}", [P, S], F32) for t in range(PACK)]
+
+        def stage1(h, t):
+            cols = slice(h * HALF, (h + 1) * HALF)
+            nc.scalar.activation(sig[h][:, t, :], y[t][:].indirect(entries(n1_t, cols.start, cols.stop)), ACT.Sigmoid)
+            nc.vector.tensor_copy(got[h][:, t, :], y[t][:].indirect(entries(n2_t, cols.start, cols.stop)))
+
+        def gate(h, t):
+            cols = slice(h * HALF, (h + 1) * HALF)
+            nc.vector.tensor_tensor(gated[h][:, t, :], y[t][:, cols], sig[h][:, t, :], ALU.mult)
+
+        def finish1(h, copy):
+            cols = slice(h * HALF, (h + 1) * HALF)
+            nc.vector.tensor_tensor(larger[h][:], gated[h][:], got[h][:], ALU.max)
+            for t in range(PACK):
+                nc.scalar.activation(zp[h][:, t, :], larger[h][:, t, :], ACT.Copy, scale=gs_t[:, t : t + 1])
+            interleave(copy, zi[h], zp[h])
+
+        def quant1(h):
+            cols = slice(h * HALF, (h + 1) * HALF)
+            nc.vector.quantize_mx(out=zw[:, cols].bitcast(FP8X4), scales=zs[:, cols], in_=zi[h][:])
+            for t in range(PACK):
+                product(a_ps[t][:, cols], ca_wd, ca_sd, t, zw[:, cols], zs[:, cols])
+                nc.scalar.activation(a_half[t][:, cols], a_ps[t][:, cols], ACT.Copy, scale=-0.03125)
+                nc.scalar.activation(a_full[t][:, cols], a_ps[t][:, cols], ACT.Copy, scale=0.0625)
+
+        for t in range(PACK):
+            y_ps = psum.tile([P, S], F32, name=f"y_ps{t}", tag=f"yb{t}")
+            product(y_ps[:], ww_d, ws_d, t, xq_w[:], xq_s[:])
+            nc.scalar.copy(y[t][:], y_ps[:])
+            stage1(0, t)
+            if t > 0:
+                gate(0, t - 1)
+        gate(0, PACK - 1)
+        stage1(1, 0)
+        finish1(0, nc.scalar.copy)
+        for t in range(1, PACK):
+            stage1(1, t)
+            gate(1, t - 1)
+        gate(1, PACK - 1)
+        quant1(0)
+        finish1(1, nc.vector.tensor_copy)
+        cb_w = pick("cb_w", xw, U32, cb_t)
+        quant1(1)
+        cb_wd = dealt("cb_wd", cb_w, U32, 4)
+        cb_sd = dealt("cb_sd", cb_s, U8, 16)
+
+        b = [new(f"b{t}", [P, S], F32) for t in range(PACK)]
+        for t in range(PACK):
+            b_ps = psum.tile([P, S], F32, name=f"b_ps{t}", tag=f"yb{t}")
+            product(b_ps[:], cb_wd, cb_sd, t, zw[:], zs[:])
+            nc.scalar.activation(b[t][:], b_ps[:], ACT.Copy, scale=0.0625)
+
+        ow = new("ow", [P, S], U32)
+        osc = new("osc", [P, S], U8)
+        out_rows = out_0.rearrange("(p t) c -> p t c", t=PACK)
+        out_words = out_1[0].rearrange("p n t -> p (n t)").bitcast(I32)
+        diff, low, high, small, res, resi = [], [], [], [], [], []
+        for k, (lo, hi) in enumerate(OUT_CHUNKS):
+            for lst, nm in ((diff, "diff"), (low, "low"), (high, "high"), (small, "small"), (res, "res")):
+                lst.append(new(f"{nm}{k}", [P, PACK, hi - lo], F32))
+            resi.append(new(f"resi{k}", [P, PACK * (hi - lo)], BF16))
+        for k, (lo, hi) in enumerate(OUT_CHUNKS):
+            for t in range(PACK):
+                nc.vector.tensor_tensor(diff[k][:, t, :], a_half[t][:].indirect(entries(n3_t, lo, hi)), a_full[t][:, lo:hi], ALU.add)
+
+        def fetch(dst, lst, k, t):
+            lo, hi = OUT_CHUNKS[k]
+            nc.vector.tensor_copy(dst[k][:, t, :], b[t][:].indirect(entries(lst, lo, hi)))
+
+        def finish2(k, copy):
+            lo, hi = OUT_CHUNKS[k]
+            nc.vector.tensor_tensor(res[k][:], small[k][:], high[k][:], ALU.max)
+            nc.sync.dma_start(out_rows[:, :, lo:hi], res[k][:])
+            interleave(copy, resi[k], res[k])
+
+        def quant2(k):
+            lo, hi = OUT_CHUNKS[k]
+            nc.vector.quantize_mx(out=ow[:, lo:hi].bitcast(FP8X4), scales=osc[:, lo:hi], in_=resi[k][:])
+            nc.sync.dma_start(out_words[:, lo:hi], ow[:, lo:hi].bitcast(I32))
+
+        last = len(OUT_CHUNKS) - 1
+        for k in range(len(OUT_CHUNKS)):
+            fetch(low, n4_t, k, 0)
+            if k > 0:
+                finish2(k - 1, nc.scalar.copy)
+            for t in range(1, PACK):
+                fetch(low, n4_t, k, t)
+            fetch(high, n5_t, k, 0)
+            fetch(high, n5_t, k, 1)
+            nc.vector.tensor_tensor(small[k][:], diff[k][:], low[k][:], ALU.min)
+            fetch(high, n5_t, k, 2)
+            fetch(high, n5_t, k, 3)
+            if k > 0:
+                quant2(k - 1)
+        finish2(last, nc.vector.tensor_copy)
+        quant2(last)
+        for q in range(4):
+            queue = nc.scalar if q % 2 else nc.sync
+            queue.dma_start(out_2[0, 4 * q : 4 * q + 4, :].bitcast(I32), osc[32 * q : 32 * q + 4, :].bitcast(I32))

@@ -1,6 +1,7 @@
 from contextlib import ExitStack
 
 import concourse.mybir as mybir
+from concourse.masks import make_identity
 
 F32 = mybir.dt.float32
 BF16 = mybir.dt.bfloat16
@@ -18,7 +19,6 @@ T = 2048
 S = 512
 HALF = S // 2
 FLOPS = 3 * 2 * 512 * 512 * 512
-OUT_CHUNKS = ((0, 256), (256, 384), (384, 512))
 
 
 def tile_picked_ccmpclampbgmax_none_po_kernel(tc, x_words, x_scales, w1_words, w1_scales, gs, offs, n1, n2, ca, cb, n3, n4, n5, out_0, out_1, out_2):
@@ -27,17 +27,17 @@ def tile_picked_ccmpclampbgmax_none_po_kernel(tc, x_words, x_scales, w1_words, w
         keep = ctx.enter_context(tc.tile_pool(name="keep", bufs=1))
         psum = ctx.enter_context(tc.psum_pool(name="psum", bufs=1))
 
-        def new(name, shape, dtype):
-            return keep.tile(shape, dtype, name=name, align_bytes=64)
+        def new(name, shape, dtype, tag=None):
+            return keep.tile(shape, dtype, name=name, tag=tag or name, align_bytes=64)
 
         def load_list(name, src):
             tile = keep.tile([P, S // 16], U16, name=name)
             nc.sync.dma_start(tile[:], src)
             return tile
 
-        def load_scales(tile, src):
+        def load_scales(queue, tile, src):
             for q in range(4):
-                nc.sync.dma_start(tile[32 * q : 32 * q + 4, :].bitcast(I32), src[0, 4 * q : 4 * q + 4, :].bitcast(I32))
+                queue.dma_start(tile[32 * q : 32 * q + 4, :].bitcast(I32), src[0, 4 * q : 4 * q + 4, :].bitcast(I32))
 
         def load_words(tile, src):
             nc.sync.dma_start(tile[:].bitcast(I32), src[0].rearrange("p n t -> p (n t)").bitcast(I32))
@@ -52,26 +52,33 @@ def tile_picked_ccmpclampbgmax_none_po_kernel(tc, x_words, x_scales, w1_words, w
             return tile[:, lo // 16 : hi // 16]
 
         def interleave(copy, dst, src):
-            copy(dst[:].rearrange("p (c i t) -> p c t i", t=PACK, i=4), src[:].rearrange("p t (c i) -> p c t i", i=4))
+            copy(dst[:].rearrange("p (c i t) -> p c t i", t=PACK, i=4), src.rearrange("p t (c i) -> p c t i", i=4))
 
         xs = new("xs", [P, T], U8)
         ws = new("ws", [P, S], U8)
-        nc.vector.memset(xs[:].bitcast(I32), 0)
+        nc.gpsimd.memset(xs[:].bitcast(I32), 0)
+        ident = new("ident", [P, P], F32)
+        make_identity(nc, ident[:])
         nc.gpsimd.memset(ws[:].bitcast(I32), 0)
         warm = new("warm", [P, 1], F32)
         warm_out = new("warm_out", [P, 1], F32)
-        nc.gpsimd.memset(warm[:], 0.0)
+        nc.vector.memset(warm[:], 0.0)
         nc.scalar.activation(warm_out[:], warm[:], ACT.Sigmoid)
+
+        a_win = [new(f"a_win{t}", [P, 2 * S], F32) for t in range(PACK)]
+        b_win = [new(f"b_win{t}", [P, 2 * S], F32) for t in range(PACK)]
+        for t in range(PACK):
+            nc.vector.memset(a_win[t][:, S:], 0.0)
 
         offs_t = load_list("offs_t", offs)
         ca_t = load_list("ca_t", ca)
         cb_t = load_list("cb_t", cb)
-        load_scales(xs, x_scales)
+        load_scales(nc.sync, xs, x_scales)
         xw = new("xw", [P, T], U32)
         load_words(xw, x_words)
         ww = new("ww", [P, S], U32)
         load_words(ww, w1_words)
-        load_scales(ws, w1_scales)
+        load_scales(nc.sync, ws, w1_scales)
         n1_t = load_list("n1_t", n1)
         n2_t = load_list("n2_t", n2)
         gs_t = new("gs_t", [P, PACK], F32)
@@ -80,18 +87,14 @@ def tile_picked_ccmpclampbgmax_none_po_kernel(tc, x_words, x_scales, w1_words, w
         n4_t = load_list("n4_t", n4)
         n5_t = load_list("n5_t", n5)
 
-        ww_d = new("ww_d", [P, S], U32)
-        ws_d = new("ws_d", [P, S], U8)
-        deal(nc.gpsimd, ww_d, ww, 4)
-        deal(nc.gpsimd, ws_d, ws, 16)
 
-        def pick(name, table, dtype, lst):
-            tile = new(name, [P, S], dtype)
+        def pick(name, table, dtype, lst, tag=None):
+            tile = new(name, [P, S], dtype, tag)
             nc.vector.tensor_copy(tile[:], table[:].indirect(lst[:]))
             return tile
 
-        def dealt(name, tile, dtype, run):
-            res = new(name, [P, S], dtype)
+        def dealt(name, tile, dtype, run, tag=None):
+            res = new(name, [P, S], dtype, tag)
             deal(nc.vector, res, tile, run)
             return res
 
@@ -99,123 +102,139 @@ def tile_picked_ccmpclampbgmax_none_po_kernel(tc, x_words, x_scales, w1_words, w
         ca_s = pick("ca_s", xs, U8, ca_t)
         cb_s = pick("cb_s", xs, U8, cb_t)
         xq_w = pick("xq_w", xw, U32, offs_t)
-        ca_w = pick("ca_w", xw, U32, ca_t)
+        ww_d = dealt("ww_d", ww, U32, 4)
+        ws_d = dealt("ws_d", ws, U8, 16)
+        ca_w = pick("ca_w", xw, U32, ca_t, "ws")
         ca_wd = dealt("ca_wd", ca_w, U32, 4)
-        ca_sd = dealt("ca_sd", ca_s, U8, 16)
+        ca_sd = dealt("ca_sd", ca_s, U8, 16, "ww")
 
         def product(dst, lw, ls, t, rw, rs):
             cols = slice(P * t, P * (t + 1))
             nc.tensor.matmul_mx(out=dst, lhsT=lw[:, cols].bitcast(FP8X4), lhsT_scale=ls[:, cols],
                                 rhs=rw.bitcast(FP8X4), rhs_scale=rs, start=True, stop=True)
 
-        y = [new(f"y{t}", [P, S], F32) for t in range(PACK)]
-        sig = [new(f"sig{h}", [P, PACK, HALF], F32) for h in range(2)]
-        got = [new(f"got{h}", [P, PACK, HALF], F32) for h in range(2)]
-        gated = [new(f"gated{h}", [P, PACK, HALF], F32) for h in range(2)]
-        larger = [new(f"larger{h}", [P, PACK, HALF], F32) for h in range(2)]
-        zp = [new(f"zp{h}", [P, PACK, HALF], BF16) for h in range(2)]
-        zi = [new(f"zi{h}", [P, PACK * HALF], BF16) for h in range(2)]
-        zw = new("zw", [P, S], U32)
-        zs = new("zs", [P, S], U8)
-        a_ps = [psum.tile([P, S], F32, name=f"a_ps{t}") for t in range(PACK)]
-        a_half = [new(f"a_half{t}", [P, S], F32) for t in range(PACK)]
-        a_full = [new(f"a_full{t}", [P, S], F32) for t in range(PACK)]
+        zp = new("zp", [P, PACK, S], BF16)
+        sig, got, gated = {}, {}, {}
 
-        def stage1(h, t):
-            cols = slice(h * HALF, (h + 1) * HALF)
-            nc.scalar.activation(sig[h][:, t, :], y[t][:].indirect(entries(n1_t, cols.start, cols.stop)), ACT.Sigmoid)
-            nc.vector.tensor_copy(got[h][:, t, :], y[t][:].indirect(entries(n2_t, cols.start, cols.stop)))
+        def gate(t):
+            gated[t] = new(f"gated{t}", [P, S], F32)
+            nc.vector.tensor_tensor(gated[t][:], a_win[t][:, :S], sig[t][:], ALU.mult)
 
-        def gate(h, t):
-            cols = slice(h * HALF, (h + 1) * HALF)
-            nc.vector.tensor_tensor(gated[h][:, t, :], y[t][:, cols], sig[h][:, t, :], ALU.mult)
-
-        def finish1(h, copy):
-            cols = slice(h * HALF, (h + 1) * HALF)
-            nc.vector.tensor_tensor(larger[h][:], gated[h][:], got[h][:], ALU.max)
-            for t in range(PACK):
-                nc.scalar.activation(zp[h][:, t, :], larger[h][:, t, :], ACT.Copy, scale=gs_t[:, t : t + 1])
-            interleave(copy, zi[h], zp[h])
-
-        def quant1(h):
-            cols = slice(h * HALF, (h + 1) * HALF)
-            nc.vector.quantize_mx(out=zw[:, cols].bitcast(FP8X4), scales=zs[:, cols], in_=zi[h][:])
-            for t in range(PACK):
-                product(a_ps[t][:, cols], ca_wd, ca_sd, t, zw[:, cols], zs[:, cols])
-                nc.scalar.activation(a_half[t][:, cols], a_ps[t][:, cols], ACT.Copy, scale=-0.03125)
-                nc.scalar.activation(a_full[t][:, cols], a_ps[t][:, cols], ACT.Copy, scale=0.0625)
+        def weigh(t):
+            larger = new(f"larger{t}", [P, S], F32)
+            nc.vector.tensor_tensor(larger[:], gated[t][:], got[t][:], ALU.max)
+            nc.scalar.activation(zp[:, t, :], larger[:], ACT.Copy, scale=gs_t[:, t : t + 1])
 
         for t in range(PACK):
             y_ps = psum.tile([P, S], F32, name=f"y_ps{t}", tag=f"yb{t}")
             product(y_ps[:], ww_d, ws_d, t, xq_w[:], xq_s[:])
-            nc.scalar.copy(y[t][:], y_ps[:])
-            stage1(0, t)
+            nc.scalar.copy(a_win[t][:, :S], y_ps[:])
+            sig[t] = new(f"sig{t}", [P, S], F32)
+            nc.scalar.activation(sig[t][:], a_win[t][:].indirect(n1_t[:]), ACT.Sigmoid)
+            got[t] = new(f"got{t}", [P, S], F32)
+            nc.vector.tensor_copy(got[t][:], a_win[t][:].indirect(n2_t[:]))
+            if t > 1:
+                weigh(t - 2)
             if t > 0:
-                gate(0, t - 1)
-        gate(0, PACK - 1)
-        stage1(1, 0)
-        finish1(0, nc.scalar.copy)
-        for t in range(1, PACK):
-            stage1(1, t)
-            gate(1, t - 1)
-        gate(1, PACK - 1)
-        quant1(0)
-        finish1(1, nc.vector.tensor_copy)
-        cb_w = pick("cb_w", xw, U32, cb_t)
-        quant1(1)
-        cb_wd = dealt("cb_wd", cb_w, U32, 4)
-        cb_sd = dealt("cb_sd", cb_s, U8, 16)
+                gate(t - 1)
+        weigh(PACK - 2)
+        gate(PACK - 1)
+        weigh(PACK - 1)
+        cb_w = pick("cb_w", xw, U32, cb_t, "gated3")
 
-        b = [new(f"b{t}", [P, S], F32) for t in range(PACK)]
+        zw = new("zw", [P, S], U32)
+        zs = new("zs", [P, S], U8)
+        zi = [new(f"zi{h}", [P, PACK * HALF], BF16) for h in range(2)]
+        interleave(nc.vector.tensor_copy, zi[0], zp[:, :, :HALF])
+        interleave(nc.scalar.copy, zi[1], zp[:, :, HALF:])
+        a_ps = {}
+        for h in range(2):
+            cols = slice(h * HALF, (h + 1) * HALF)
+            nc.vector.quantize_mx(out=zw[:, cols].bitcast(FP8X4), scales=zs[:, cols], in_=zi[h][:])
+            for t in range(PACK):
+                a_ps[h, t] = psum.tile([P, HALF], F32, name=f"a_ps{h}{t}", tag=f"{'ya'[h]}b{t}")
+                product(a_ps[h, t][:], ca_wd, ca_sd, t, zw[:, cols], zs[:, cols])
+        cb_wd = dealt("cb_wd", cb_w, U32, 4, "zi1")
+        cb_sd = dealt("cb_sd", cb_s, U8, 16, "zi0")
+        for t in range(PACK):
+            for h in range(2):
+                lo, hi = h * HALF, (h + 1) * HALF
+                nc.scalar.activation(a_win[t][:, lo:hi], a_ps[h, t][:], ACT.Copy, scale=0.03125)
+                nc.scalar.activation(b_win[t][:, S + lo : S + hi], a_ps[h, t][:], ACT.Copy, scale=-0.0625)
+
         for t in range(PACK):
             b_ps = psum.tile([P, S], F32, name=f"b_ps{t}", tag=f"yb{t}")
             product(b_ps[:], cb_wd, cb_sd, t, zw[:], zs[:])
-            nc.scalar.activation(b[t][:], b_ps[:], ACT.Copy, scale=0.0625)
+            nc.scalar.activation(b_win[t][:, :S], b_ps[:], ACT.Copy, scale=0.0625)
 
         ow = new("ow", [P, S], U32)
         osc = new("osc", [P, S], U8)
         out_rows = out_0.rearrange("(p t) c -> p t c", t=PACK)
         out_words = out_1[0].rearrange("p n t -> p (n t)").bitcast(I32)
-        diff, low, high, small, res, resi = [], [], [], [], [], []
-        for k, (lo, hi) in enumerate(OUT_CHUNKS):
-            for lst, nm in ((diff, "diff"), (low, "low"), (high, "high"), (small, "small"), (res, "res")):
-                lst.append(new(f"{nm}{k}", [P, PACK, hi - lo], F32))
-            resi.append(new(f"resi{k}", [P, PACK * (hi - lo)], BF16))
-        for k, (lo, hi) in enumerate(OUT_CHUNKS):
-            for t in range(PACK):
-                nc.vector.tensor_tensor(diff[k][:, t, :], a_half[t][:].indirect(entries(n3_t, lo, hi)), a_full[t][:, lo:hi], ALU.add)
+        neg = [new(f"neg{t}", [P, S], F32) for t in range(PACK)]
+        for t in range(PACK):
+            nc.vector.tensor_tensor(neg[t][:], a_win[t][:].indirect(n3_t[:]), b_win[t][:, S:], ALU.add)
+        back = [[psum.tile([P, 2, HALF], F32, name=f"back{h}{u}", tag=f"yb{2 * u + h}") for u in range(2)] for h in range(2)]
+        for t in range(PACK):
+            gap = new(f"gap{t}", [P, S], F32)
+            nc.vector.tensor_tensor(gap[:], b_win[t][:].indirect(n4_t[:]), neg[t][:], ALU.add)
+            over = new(f"over{t}", [P, S], F32)
+            nc.scalar.activation(over[:], gap[:], ACT.Relu, scale=-1.0)
+            turned_ps = psum.tile([P, S], F32, name=f"turned_ps{t}", tag=f"ab{t}")
+            for k in range(PACK):
+                cols = slice(P * k, P * (k + 1))
+                nc.tensor.matmul(turned_ps[:, cols], neg[t][:, cols], ident[:], start=True, stop=False, is_transpose=True)
+                nc.tensor.matmul(turned_ps[:, cols], over[:, cols], ident[:], start=False, stop=True, is_transpose=True)
+            turned = new(f"turned{t}", [P, S], F32)
+            nc.scalar.copy(turned[:], turned_ps[:])
+            for k in range(PACK):
+                nc.tensor.transpose(back[k // 2][t // 2][:, t % 2, P * (k % 2) : P * (k % 2 + 1)], turned[:, P * k : P * (k + 1)], ident[:])
 
-        def fetch(dst, lst, k, t):
-            lo, hi = OUT_CHUNKS[k]
-            nc.vector.tensor_copy(dst[k][:, t, :], b[t][:].indirect(entries(lst, lo, hi)))
+        res = [new(f"res{h}", [P, PACK, HALF], F32) for h in range(2)]
 
-        def finish2(k, copy):
-            lo, hi = OUT_CHUNKS[k]
-            nc.vector.tensor_tensor(res[k][:], small[k][:], high[k][:], ALU.max)
-            nc.sync.dma_start(out_rows[:, :, lo:hi], res[k][:])
-            interleave(copy, resi[k], res[k])
+        def fetch(h, u, tag=None):
+            tile = new(f"high{h}{u}", [P, 2, HALF], F32, tag)
+            for e in range(2):
+                nc.vector.tensor_copy(tile[:, e, :], b_win[2 * u + e][:].indirect(entries(n5_t, h * HALF, (h + 1) * HALF)))
+            return tile
 
-        def quant2(k):
-            lo, hi = OUT_CHUNKS[k]
-            nc.vector.quantize_mx(out=ow[:, lo:hi].bitcast(FP8X4), scales=osc[:, lo:hi], in_=resi[k][:])
-            nc.sync.dma_start(out_words[:, lo:hi], ow[:, lo:hi].bitcast(I32))
+        def finish2(h, u, high, cols):
+            nc.vector.scalar_tensor_tensor(res[h][:, 2 * u : 2 * u + 2, cols], back[h][u][:, :, cols], -1.0, high[:, :, cols], ALU.mult, ALU.max)
 
-        last = len(OUT_CHUNKS) - 1
-        for k in range(len(OUT_CHUNKS)):
-            fetch(low, n4_t, k, 0)
-            if k > 0:
-                finish2(k - 1, nc.scalar.copy)
-            for t in range(1, PACK):
-                fetch(low, n4_t, k, t)
-            fetch(high, n5_t, k, 0)
-            fetch(high, n5_t, k, 1)
-            nc.vector.tensor_tensor(small[k][:], diff[k][:], low[k][:], ALU.min)
-            fetch(high, n5_t, k, 2)
-            fetch(high, n5_t, k, 3)
-            if k > 0:
-                quant2(k - 1)
-        finish2(last, nc.vector.tensor_copy)
-        quant2(last)
+        def store(h, u):
+            rows = slice(2 * u, 2 * u + 2)
+            nc.sync.dma_start(out_rows[:, rows, h * HALF : (h + 1) * HALF], res[h][:, rows, :])
+
+        def quant2(lo, hi, resi):
+            nc.vector.quantize_mx(out=ow[:, lo:hi].bitcast(FP8X4), scales=osc[:, lo:hi], in_=resi[:])
+
+        def round2(name, src, width, copy):
+            resi = new(name, [P, PACK * width], BF16)
+            interleave(copy, resi, src)
+            return resi
+
+        whole = slice(0, HALF)
+        high00 = fetch(0, 0)
+        high01 = fetch(0, 1)
+        finish2(0, 0, high00, whole)
+        store(0, 0)
+        high10 = fetch(1, 0)
+        finish2(0, 1, high01, whole)
+        store(0, 1)
+        r0 = round2("r0", res[0][:], HALF, nc.scalar.copy)
+        finish2(1, 0, high10, whole)
+        store(1, 0)
+        high11 = fetch(1, 1, "high01")
+        quant2(0, HALF, r0)
+        nc.sync.dma_start(out_words[:, :HALF], ow[:, :HALF].bitcast(I32))
+        finish2(1, 1, high11, slice(0, P))
+        r1 = round2("r1", res[1][:, :, :P], P, nc.scalar.copy)
+        finish2(1, 1, high11, slice(P, HALF))
+        store(1, 1)
+        r2 = round2("r2", res[1][:, :, P:], P, nc.vector.tensor_copy)
+        quant2(HALF, HALF + P, r1)
+        quant2(HALF + P, S, r2)
+        nc.sync.dma_start(out_words[:, HALF:], ow[:, HALF:].bitcast(I32))
         for q in range(4):
-            queue = nc.scalar if q % 2 else nc.sync
+            queue = nc.sync if q % 2 else nc.scalar
             queue.dma_start(out_2[0, 4 * q : 4 * q + 4, :].bitcast(I32), osc[32 * q : 32 * q + 4, :].bitcast(I32))

@@ -72,12 +72,12 @@ def tile_picked_ccmpclampbgmax_none_po_kernel(tc, x_words, x_scales, w1_words, w
 
         offs_t = load_list("offs_t", offs)
         ca_t = load_list("ca_t", ca)
-        cb_t = load_list("cb_t", cb)
         load_scales(nc.sync, xs, x_scales)
-        xw = new("xw", [P, T], U32)
-        load_words(xw, x_words)
         ww = new("ww", [P, S], U32)
         load_words(ww, w1_words)
+        xw = new("xw", [P, T], U32)
+        load_words(xw, x_words)
+        cb_t = load_list("cb_t", cb)
         load_scales(nc.sync, ws, w1_scales)
         n1_t = load_list("n1_t", n1)
         n2_t = load_list("n2_t", n2)
@@ -93,6 +93,11 @@ def tile_picked_ccmpclampbgmax_none_po_kernel(tc, x_words, x_scales, w1_words, w
             nc.vector.tensor_copy(tile[:], table[:].indirect(lst[:]))
             return tile
 
+        def pick_dealt(name, lst, tag=None):
+            tile = new(name, [P, S], U32, tag)
+            nc.vector.tensor_copy(tile[:].rearrange("p (t m) -> p m t", t=PACK), xw[:].indirect(lst[:]))
+            return tile
+
         def dealt(name, tile, dtype, run, tag=None):
             res = new(name, [P, S], dtype, tag)
             deal(nc.vector, res, tile, run)
@@ -102,11 +107,12 @@ def tile_picked_ccmpclampbgmax_none_po_kernel(tc, x_words, x_scales, w1_words, w
         ca_s = pick("ca_s", xs, U8, ca_t)
         cb_s = pick("cb_s", xs, U8, cb_t)
         xq_w = pick("xq_w", xw, U32, offs_t)
-        ww_d = dealt("ww_d", ww, U32, 4)
-        ws_d = dealt("ws_d", ws, U8, 16)
-        ca_w = pick("ca_w", xw, U32, ca_t, "ws")
-        ca_wd = dealt("ca_wd", ca_w, U32, 4)
-        ca_sd = dealt("ca_sd", ca_s, U8, 16, "ww")
+        ww_d = new("ww_d", [P, S], U32)
+        ws_d = new("ws_d", [P, S], U8)
+        deal(nc.gpsimd, ww_d, ww, 4)
+        deal(nc.gpsimd, ws_d, ws, 16)
+        ca_wd = pick_dealt("ca_wd", ca_t)
+        ca_sd = dealt("ca_sd", ca_s, U8, 16)
 
         def product(dst, lw, ls, t, rw, rs):
             cols = slice(P * t, P * (t + 1))
@@ -140,8 +146,8 @@ def tile_picked_ccmpclampbgmax_none_po_kernel(tc, x_words, x_scales, w1_words, w
         weigh(PACK - 2)
         gate(PACK - 1)
         weigh(PACK - 1)
-        cb_w = pick("cb_w", xw, U32, cb_t, "gated3")
 
+        cb_sd = dealt("cb_sd", cb_s, U8, 16, "gated3")
         zw = new("zw", [P, S], U32)
         zs = new("zs", [P, S], U8)
         zi = [new(f"zi{h}", [P, PACK * HALF], BF16) for h in range(2)]
@@ -154,41 +160,64 @@ def tile_picked_ccmpclampbgmax_none_po_kernel(tc, x_words, x_scales, w1_words, w
             for t in range(PACK):
                 a_ps[h, t] = psum.tile([P, HALF], F32, name=f"a_ps{h}{t}", tag=f"{'ya'[h]}b{t}")
                 product(a_ps[h, t][:], ca_wd, ca_sd, t, zw[:, cols], zs[:, cols])
-        cb_wd = dealt("cb_wd", cb_w, U32, 4, "zi1")
-        cb_sd = dealt("cb_sd", cb_s, U8, 16, "zi0")
-        for t in range(PACK):
-            for h in range(2):
-                lo, hi = h * HALF, (h + 1) * HALF
-                nc.scalar.activation(a_win[t][:, lo:hi], a_ps[h, t][:], ACT.Copy, scale=0.03125)
-                nc.scalar.activation(b_win[t][:, S + lo : S + hi], a_ps[h, t][:], ACT.Copy, scale=-0.0625)
-
-        for t in range(PACK):
-            b_ps = psum.tile([P, S], F32, name=f"b_ps{t}", tag=f"yb{t}")
-            product(b_ps[:], cb_wd, cb_sd, t, zw[:], zs[:])
-            nc.scalar.activation(b_win[t][:, :S], b_ps[:], ACT.Copy, scale=0.0625)
+        cb_wd = pick_dealt("cb_wd", cb_t, "zi1")
 
         ow = new("ow", [P, S], U32)
         osc = new("osc", [P, S], U8)
         out_rows = out_0.rearrange("(p t) c -> p t c", t=PACK)
         out_words = out_1[0].rearrange("p n t -> p (n t)").bitcast(I32)
-        neg = [new(f"neg{t}", [P, S], F32) for t in range(PACK)]
-        for t in range(PACK):
+        neg, gap, over, back = {}, {}, {}, {}
+
+        def score_a(t):
+            for h in range(2):
+                lo, hi = h * HALF, (h + 1) * HALF
+                nc.scalar.activation(a_win[t][:, lo:hi], a_ps[h, t][:], ACT.Copy, scale=0.03125)
+                nc.scalar.activation(b_win[t][:, S + lo : S + hi], a_ps[h, t][:], ACT.Copy, scale=-0.0625)
+            neg[t] = new(f"neg{t}", [P, S], F32)
             nc.vector.tensor_tensor(neg[t][:], a_win[t][:].indirect(n3_t[:]), b_win[t][:, S:], ALU.add)
-        back = [[psum.tile([P, 2, HALF], F32, name=f"back{h}{u}", tag=f"yb{2 * u + h}") for u in range(2)] for h in range(2)]
-        for t in range(PACK):
-            gap = new(f"gap{t}", [P, S], F32)
-            nc.vector.tensor_tensor(gap[:], b_win[t][:].indirect(n4_t[:]), neg[t][:], ALU.add)
-            over = new(f"over{t}", [P, S], F32)
-            nc.scalar.activation(over[:], gap[:], ACT.Relu, scale=-1.0)
+
+        def score_b(t):
+            b_ps = psum.tile([P, S], F32, name=f"b_ps{t}", tag=f"yb{t}")
+            product(b_ps[:], cb_wd, cb_sd, t, zw[:], zs[:])
+            nc.scalar.activation(b_win[t][:, :S], b_ps[:], ACT.Copy, scale=0.0625)
+            gap[t] = new(f"gap{t}", [P, S], F32)
+            nc.vector.tensor_tensor(gap[t][:], b_win[t][:].indirect(n4_t[:]), neg[t][:], ALU.add)
+
+        def clip(t):
+            over[t] = new(f"over{t}", [P, S], F32)
+            nc.scalar.activation(over[t][:], gap[t][:], ACT.Relu, scale=-1.0)
+
+        def turn(t):
             turned_ps = psum.tile([P, S], F32, name=f"turned_ps{t}", tag=f"ab{t}")
             for k in range(PACK):
                 cols = slice(P * k, P * (k + 1))
                 nc.tensor.matmul(turned_ps[:, cols], neg[t][:, cols], ident[:], start=True, stop=False, is_transpose=True)
-                nc.tensor.matmul(turned_ps[:, cols], over[:, cols], ident[:], start=False, stop=True, is_transpose=True)
+                nc.tensor.matmul(turned_ps[:, cols], over[t][:, cols], ident[:], start=False, stop=True, is_transpose=True)
             turned = new(f"turned{t}", [P, S], F32)
             nc.scalar.copy(turned[:], turned_ps[:])
+            u = t // 2
             for k in range(PACK):
-                nc.tensor.transpose(back[k // 2][t // 2][:, t % 2, P * (k % 2) : P * (k % 2 + 1)], turned[:, P * k : P * (k + 1)], ident[:])
+                h = k // 2
+                if (h, u) not in back:
+                    back[h, u] = psum.tile([P, 2, HALF], F32, name=f"back{h}{u}", tag=f"yb{2 * u + h}")
+                nc.tensor.transpose(back[h, u][:, t % 2, P * (k % 2) : P * (k % 2 + 1)], turned[:, P * k : P * (k + 1)], ident[:])
+
+        score_a(0)
+        score_a(1)
+        score_b(0)
+        score_a(2)
+        score_b(1)
+        clip(0)
+        score_a(3)
+        score_b(2)
+        turn(0)
+        clip(1)
+        score_b(3)
+        clip(2)
+        turn(1)
+        clip(3)
+        turn(2)
+        turn(3)
 
         res = [new(f"res{h}", [P, PACK, HALF], F32) for h in range(2)]
 
@@ -199,7 +228,7 @@ def tile_picked_ccmpclampbgmax_none_po_kernel(tc, x_words, x_scales, w1_words, w
             return tile
 
         def finish2(h, u, high, cols):
-            nc.vector.scalar_tensor_tensor(res[h][:, 2 * u : 2 * u + 2, cols], back[h][u][:, :, cols], -1.0, high[:, :, cols], ALU.mult, ALU.max)
+            nc.vector.scalar_tensor_tensor(res[h][:, 2 * u : 2 * u + 2, cols], back[h, u][:, :, cols], -1.0, high[:, :, cols], ALU.mult, ALU.max)
 
         def store(h, u):
             rows = slice(2 * u, 2 * u + 2)
@@ -214,17 +243,17 @@ def tile_picked_ccmpclampbgmax_none_po_kernel(tc, x_words, x_scales, w1_words, w
             return resi
 
         whole = slice(0, HALF)
-        high00 = fetch(0, 0)
-        high01 = fetch(0, 1)
+        high00 = fetch(0, 0, "gap2")
+        high10 = fetch(1, 0, "gap3")
         finish2(0, 0, high00, whole)
         store(0, 0)
-        high10 = fetch(1, 0)
+        high01 = fetch(0, 1, "over2")
+        finish2(1, 0, high10, whole)
+        store(1, 0)
         finish2(0, 1, high01, whole)
         store(0, 1)
         r0 = round2("r0", res[0][:], HALF, nc.scalar.copy)
-        finish2(1, 0, high10, whole)
-        store(1, 0)
-        high11 = fetch(1, 1, "high01")
+        high11 = fetch(1, 1, "over2")
         quant2(0, HALF, r0)
         nc.sync.dma_start(out_words[:, :HALF], ow[:, :HALF].bitcast(I32))
         finish2(1, 1, high11, slice(0, P))

@@ -60,11 +60,11 @@ def tile_picked_ccmpclampbgmax_none_po_kernel(tc, x_words, x_scales, w1_words, w
         ident = new("ident", [P, P], F32)
         make_identity(nc, ident[:])
         nc.gpsimd.memset(ws[:].bitcast(I32), 0)
+
         warm = new("warm", [P, 1], F32)
         warm_out = new("warm_out", [P, 1], F32)
         nc.vector.memset(warm[:], 0.0)
         nc.scalar.activation(warm_out[:], warm[:], ACT.Sigmoid)
-
         a_win = [new(f"a_win{t}", [P, 2 * S], F32) for t in range(PACK)]
         b_win = [new(f"b_win{t}", [P, 2 * S], F32) for t in range(PACK)]
         for t in range(PACK):
@@ -126,8 +126,8 @@ def tile_picked_ccmpclampbgmax_none_po_kernel(tc, x_words, x_scales, w1_words, w
             gated[t] = new(f"gated{t}", [P, S], F32)
             nc.vector.tensor_tensor(gated[t][:], a_win[t][:, :S], sig[t][:], ALU.mult)
 
-        def weigh(t):
-            larger = new(f"larger{t}", [P, S], F32)
+        def weigh(t, tag=None):
+            larger = new(f"larger{t}", [P, S], F32, tag)
             nc.vector.tensor_tensor(larger[:], gated[t][:], got[t][:], ALU.max)
             nc.scalar.activation(zp[:, t, :], larger[:], ACT.Copy, scale=gs_t[:, t : t + 1])
 
@@ -143,23 +143,25 @@ def tile_picked_ccmpclampbgmax_none_po_kernel(tc, x_words, x_scales, w1_words, w
                 weigh(t - 2)
             if t > 0:
                 gate(t - 1)
-        weigh(PACK - 2)
-        gate(PACK - 1)
-        weigh(PACK - 1)
+        last = PACK - 1
+        gate(last)
+        weigh(last - 1, f"sig{last}")
+        halves = [slice(h * HALF, (h + 1) * HALF) for h in range(2)]
+        larger = new("larger_last", [P, S], F32)
+        for cols in halves:
+            nc.vector.tensor_tensor(larger[:, cols], gated[last][:, cols], got[last][:, cols], ALU.max)
+        for cols in halves:
+            nc.vector.tensor_scalar(zp[:, last, cols], larger[:, cols], gs_t[:, last:], None, ALU.mult)
 
-        cb_sd = dealt("cb_sd", cb_s, U8, 16, "gated3")
         zw = new("zw", [P, S], U32)
         zs = new("zs", [P, S], U8)
         zi = [new(f"zi{h}", [P, PACK * HALF], BF16) for h in range(2)]
         interleave(nc.vector.tensor_copy, zi[0], zp[:, :, :HALF])
         interleave(nc.scalar.copy, zi[1], zp[:, :, HALF:])
-        a_ps = {}
+        cb_sd = dealt("cb_sd", cb_s, U8, 16, "larger_last")
         for h in range(2):
             cols = slice(h * HALF, (h + 1) * HALF)
             nc.vector.quantize_mx(out=zw[:, cols].bitcast(FP8X4), scales=zs[:, cols], in_=zi[h][:])
-            for t in range(PACK):
-                a_ps[h, t] = psum.tile([P, HALF], F32, name=f"a_ps{h}{t}", tag=f"{'ya'[h]}b{t}")
-                product(a_ps[h, t][:], ca_wd, ca_sd, t, zw[:, cols], zs[:, cols])
         cb_wd = pick_dealt("cb_wd", cb_t, "zi1")
 
         ow = new("ow", [P, S], U32)
@@ -169,10 +171,12 @@ def tile_picked_ccmpclampbgmax_none_po_kernel(tc, x_words, x_scales, w1_words, w
         neg, gap, over, back = {}, {}, {}, {}
 
         def score_a(t):
-            for h in range(2):
-                lo, hi = h * HALF, (h + 1) * HALF
-                nc.scalar.activation(a_win[t][:, lo:hi], a_ps[h, t][:], ACT.Copy, scale=0.03125)
-                nc.scalar.activation(b_win[t][:, S + lo : S + hi], a_ps[h, t][:], ACT.Copy, scale=-0.0625)
+            pieces = ((0, HALF, "yb0"), (HALF, S, "ab0")) if t == 0 else ((0, S, f"ab{t}"),)
+            for lo, hi, bank in pieces:
+                a_ps = psum.tile([P, hi - lo], F32, name=f"a_ps{t}_{lo}", tag=bank)
+                product(a_ps[:], ca_wd, ca_sd, t, zw[:, lo:hi], zs[:, lo:hi])
+                nc.scalar.activation(a_win[t][:, lo:hi], a_ps[:], ACT.Copy, scale=0.03125)
+                nc.scalar.activation(b_win[t][:, S + lo : S + hi], a_ps[:], ACT.Copy, scale=-0.0625)
             neg[t] = new(f"neg{t}", [P, S], F32)
             nc.vector.tensor_tensor(neg[t][:], a_win[t][:].indirect(n3_t[:]), b_win[t][:, S:], ALU.add)
 
@@ -189,10 +193,10 @@ def tile_picked_ccmpclampbgmax_none_po_kernel(tc, x_words, x_scales, w1_words, w
 
         def turn(t):
             turned_ps = psum.tile([P, S], F32, name=f"turned_ps{t}", tag=f"ab{t}")
-            for k in range(PACK):
-                cols = slice(P * k, P * (k + 1))
-                nc.tensor.matmul(turned_ps[:, cols], neg[t][:, cols], ident[:], start=True, stop=False, is_transpose=True)
-                nc.tensor.matmul(turned_ps[:, cols], over[t][:, cols], ident[:], start=False, stop=True, is_transpose=True)
+            for j, term in enumerate((neg[t], over[t])):
+                for k in range(PACK):
+                    cols = slice(P * k, P * (k + 1))
+                    nc.tensor.matmul(turned_ps[:, cols], term[:, cols], ident[:], start=(j, k) == (0, 0), stop=(j, k) == (1, PACK - 1), is_transpose=True)
             turned = new(f"turned{t}", [P, S], F32)
             nc.scalar.copy(turned[:], turned_ps[:])
             u = t // 2
@@ -221,10 +225,10 @@ def tile_picked_ccmpclampbgmax_none_po_kernel(tc, x_words, x_scales, w1_words, w
 
         res = [new(f"res{h}", [P, PACK, HALF], F32) for h in range(2)]
 
-        def fetch(h, u, tag=None):
-            tile = new(f"high{h}{u}", [P, 2, HALF], F32, tag)
+        def fetch(u, lo, hi, tag):
+            tile = new(f"high{u}_{lo}", [P, 2, hi - lo], F32, tag)
             for e in range(2):
-                nc.vector.tensor_copy(tile[:, e, :], b_win[2 * u + e][:].indirect(entries(n5_t, h * HALF, (h + 1) * HALF)))
+                nc.vector.tensor_copy(tile[:, e, :], b_win[2 * u + e][:].indirect(entries(n5_t, lo, hi)))
             return tile
 
         def finish2(h, u, high, cols):
@@ -243,17 +247,16 @@ def tile_picked_ccmpclampbgmax_none_po_kernel(tc, x_words, x_scales, w1_words, w
             return resi
 
         whole = slice(0, HALF)
-        high00 = fetch(0, 0, "gap2")
-        high10 = fetch(1, 0, "gap3")
-        finish2(0, 0, high00, whole)
+        high0 = fetch(0, 0, S, "gap2")
+        finish2(0, 0, high0[:, :, :HALF], whole)
         store(0, 0)
-        high01 = fetch(0, 1, "over2")
-        finish2(1, 0, high10, whole)
+        high01 = fetch(1, 0, HALF, "over2")
+        finish2(1, 0, high0[:, :, HALF:], whole)
         store(1, 0)
         finish2(0, 1, high01, whole)
         store(0, 1)
         r0 = round2("r0", res[0][:], HALF, nc.scalar.copy)
-        high11 = fetch(1, 1, "over2")
+        high11 = fetch(1, HALF, S, "over2")
         quant2(0, HALF, r0)
         nc.sync.dma_start(out_words[:, :HALF], ow[:, :HALF].bitcast(I32))
         finish2(1, 1, high11, slice(0, P))

from contextlib import ExitStack

import concourse.mybir as mybir
from concourse.masks import make_identity

F32 = mybir.dt.float32
BF16 = mybir.dt.bfloat16
I32 = mybir.dt.int32
U32 = mybir.dt.uint32
U16 = mybir.dt.uint16
U8 = mybir.dt.uint8
FP8X4 = mybir.dt.float8_e4m3fn_x4
ALU = mybir.AluOpType
ACT = mybir.ActivationFunctionType

P = 128
PACK = 4
T = 2048
S = 512
HALF = S // 2
FLOPS = 3 * 2 * 512 * 512 * 512


def tile_picked_ccmpclampbgmax_none_po_kernel(tc, x_words, x_scales, w1_words, w1_scales, gs, offs, n1, n2, ca, cb, n3, n4, n5, out_0, out_1, out_2):
    nc = tc.nc
    with ExitStack() as ctx:
        keep = ctx.enter_context(tc.tile_pool(name="keep", bufs=1))
        psum = ctx.enter_context(tc.psum_pool(name="psum", bufs=1))

        def new(name, shape, dtype, tag=None):
            return keep.tile(shape, dtype, name=name, tag=tag or name, align_bytes=64)

        def load_list(name, src):
            tile = keep.tile([P, S // 16], U16, name=name)
            nc.sync.dma_start(tile[:], src)
            return tile

        def load_scales(queue, tile, src):
            for q in range(4):
                queue.dma_start(tile[32 * q : 32 * q + 4, :].bitcast(I32), src[0, 4 * q : 4 * q + 4, :].bitcast(I32))

        def load_words(tile, src):
            nc.sync.dma_start(tile[:].bitcast(I32), src[0].rearrange("p n t -> p (n t)").bitcast(I32))

        def deal(engine, dst, src, run):
            engine.tensor_copy(
                dst[:].rearrange("p (t c i) -> p c t i", t=PACK, i=run),
                src[:].rearrange("p (c i t) -> p c t i", t=PACK, i=run),
            )

        def entries(tile, lo, hi):
            return tile[:, lo // 16 : hi // 16]

        def interleave(copy, dst, src):
            copy(dst[:].rearrange("p (c i t) -> p c t i", t=PACK, i=4), src.rearrange("p t (c i) -> p c t i", i=4))

        xs = new("xs", [P, T], U8)
        ws = new("ws", [P, S], U8)
        nc.gpsimd.memset(xs[:].bitcast(I32), 0)
        ident = new("ident", [P, P], F32)
        make_identity(nc, ident[:])
        nc.gpsimd.memset(ws[:].bitcast(I32), 0)

        warm = new("warm", [P, 1], F32)
        warm_out = new("warm_out", [P, 1], F32)
        nc.vector.memset(warm[:], 0.0)
        nc.scalar.activation(warm_out[:], warm[:], ACT.Sigmoid)
        a_win = [new(f"a_win{t}", [P, 2 * S], F32) for t in range(PACK)]
        b_win = [new(f"b_win{t}", [P, 2 * S], F32) for t in range(PACK)]
        for t in range(PACK):
            nc.vector.memset(a_win[t][:, S:], 0.0)

        offs_t = load_list("offs_t", offs)
        ca_t = load_list("ca_t", ca)
        load_scales(nc.sync, xs, x_scales)
        ww = new("ww", [P, S], U32)
        load_words(ww, w1_words)
        xw = new("xw", [P, T], U32)
        load_words(xw, x_words)
        cb_t = load_list("cb_t", cb)
        load_scales(nc.sync, ws, w1_scales)
        n1_t = load_list("n1_t", n1)
        n2_t = load_list("n2_t", n2)
        gs_t = new("gs_t", [P, PACK], F32)
        nc.sync.dma_start(gs_t[:], gs.rearrange("(p t) o -> p (t o)", t=PACK))
        n3_t = load_list("n3_t", n3)
        n4_t = load_list("n4_t", n4)
        n5_t = load_list("n5_t", n5)


        def pick(name, table, dtype, lst, tag=None):
            tile = new(name, [P, S], dtype, tag)
            nc.vector.tensor_copy(tile[:], table[:].indirect(lst[:]))
            return tile

        def pick_dealt(name, lst, tag=None):
            tile = new(name, [P, S], U32, tag)
            nc.vector.tensor_copy(tile[:].rearrange("p (t m) -> p m t", t=PACK), xw[:].indirect(lst[:]))
            return tile

        def dealt(name, tile, dtype, run, tag=None):
            res = new(name, [P, S], dtype, tag)
            deal(nc.vector, res, tile, run)
            return res

        xq_s = pick("xq_s", xs, U8, offs_t)
        ca_s = pick("ca_s", xs, U8, ca_t)
        cb_s = pick("cb_s", xs, U8, cb_t)
        xq_w = pick("xq_w", xw, U32, offs_t)
        ww_d = new("ww_d", [P, S], U32)
        ws_d = new("ws_d", [P, S], U8)
        deal(nc.gpsimd, ww_d, ww, 4)
        deal(nc.gpsimd, ws_d, ws, 16)
        ca_wd = pick_dealt("ca_wd", ca_t)
        ca_sd = dealt("ca_sd", ca_s, U8, 16)

        def product(dst, lw, ls, t, rw, rs):
            cols = slice(P * t, P * (t + 1))
            nc.tensor.matmul_mx(out=dst, lhsT=lw[:, cols].bitcast(FP8X4), lhsT_scale=ls[:, cols],
                                rhs=rw.bitcast(FP8X4), rhs_scale=rs, start=True, stop=True)

        zp = new("zp", [P, PACK, S], BF16)
        sig, got, gated = {}, {}, {}

        def gate(t):
            gated[t] = new(f"gated{t}", [P, S], F32)
            nc.vector.tensor_tensor(gated[t][:], a_win[t][:, :S], sig[t][:], ALU.mult)

        def weigh(t, tag=None):
            larger = new(f"larger{t}", [P, S], F32, tag)
            nc.vector.tensor_tensor(larger[:], gated[t][:], got[t][:], ALU.max)
            nc.scalar.activation(zp[:, t, :], larger[:], ACT.Copy, scale=gs_t[:, t : t + 1])

        for t in range(PACK):
            y_ps = psum.tile([P, S], F32, name=f"y_ps{t}", tag=f"yb{t}")
            product(y_ps[:], ww_d, ws_d, t, xq_w[:], xq_s[:])
            nc.scalar.copy(a_win[t][:, :S], y_ps[:])
            sig[t] = new(f"sig{t}", [P, S], F32)
            nc.scalar.activation(sig[t][:], a_win[t][:].indirect(n1_t[:]), ACT.Sigmoid)
            got[t] = new(f"got{t}", [P, S], F32)
            nc.vector.tensor_copy(got[t][:], a_win[t][:].indirect(n2_t[:]))
            if t > 1:
                weigh(t - 2)
            if t > 0:
                gate(t - 1)
        last = PACK - 1
        gate(last)
        weigh(last - 1, f"sig{last}")
        halves = [slice(h * HALF, (h + 1) * HALF) for h in range(2)]
        larger = new("larger_last", [P, S], F32)
        for cols in halves:
            nc.vector.tensor_tensor(larger[:, cols], gated[last][:, cols], got[last][:, cols], ALU.max)
        for cols in halves:
            nc.vector.tensor_scalar(zp[:, last, cols], larger[:, cols], gs_t[:, last:], None, ALU.mult)

        zw = new("zw", [P, S], U32)
        zs = new("zs", [P, S], U8)
        zi = [new(f"zi{h}", [P, PACK * HALF], BF16) for h in range(2)]
        interleave(nc.vector.tensor_copy, zi[0], zp[:, :, :HALF])
        interleave(nc.scalar.copy, zi[1], zp[:, :, HALF:])
        cb_sd = dealt("cb_sd", cb_s, U8, 16, "larger_last")
        for h in range(2):
            cols = slice(h * HALF, (h + 1) * HALF)
            nc.vector.quantize_mx(out=zw[:, cols].bitcast(FP8X4), scales=zs[:, cols], in_=zi[h][:])
        cb_wd = pick_dealt("cb_wd", cb_t, "zi1")

        ow = new("ow", [P, S], U32)
        osc = new("osc", [P, S], U8)
        out_rows = out_0.rearrange("(p t) c -> p t c", t=PACK)
        out_words = out_1[0].rearrange("p n t -> p (n t)").bitcast(I32)
        neg, gap, over, back = {}, {}, {}, {}

        def score_a(t):
            pieces = ((0, HALF, "yb0"), (HALF, S, "ab0")) if t == 0 else ((0, S, f"ab{t}"),)
            for lo, hi, bank in pieces:
                a_ps = psum.tile([P, hi - lo], F32, name=f"a_ps{t}_{lo}", tag=bank)
                product(a_ps[:], ca_wd, ca_sd, t, zw[:, lo:hi], zs[:, lo:hi])
                nc.scalar.activation(a_win[t][:, lo:hi], a_ps[:], ACT.Copy, scale=0.03125)
                nc.scalar.activation(b_win[t][:, S + lo : S + hi], a_ps[:], ACT.Copy, scale=-0.0625)
            neg[t] = new(f"neg{t}", [P, S], F32)
            nc.vector.tensor_tensor(neg[t][:], a_win[t][:].indirect(n3_t[:]), b_win[t][:, S:], ALU.add)

        def score_b(t):
            b_ps = psum.tile([P, S], F32, name=f"b_ps{t}", tag=f"yb{t}")
            product(b_ps[:], cb_wd, cb_sd, t, zw[:], zs[:])
            nc.scalar.activation(b_win[t][:, :S], b_ps[:], ACT.Copy, scale=0.0625)
            gap[t] = new(f"gap{t}", [P, S], F32)
            nc.vector.tensor_tensor(gap[t][:], b_win[t][:].indirect(n4_t[:]), neg[t][:], ALU.add)

        def clip(t):
            over[t] = new(f"over{t}", [P, S], F32)
            nc.scalar.activation(over[t][:], gap[t][:], ACT.Relu, scale=-1.0)

        def turn(t):
            turned_ps = psum.tile([P, S], F32, name=f"turned_ps{t}", tag=f"ab{t}")
            for j, term in enumerate((neg[t], over[t])):
                for k in range(PACK):
                    cols = slice(P * k, P * (k + 1))
                    nc.tensor.matmul(turned_ps[:, cols], term[:, cols], ident[:], start=(j, k) == (0, 0), stop=(j, k) == (1, PACK - 1), is_transpose=True)
            turned = new(f"turned{t}", [P, S], F32)
            nc.scalar.copy(turned[:], turned_ps[:])
            u = t // 2
            for k in range(PACK):
                h = k // 2
                if (h, u) not in back:
                    back[h, u] = psum.tile([P, 2, HALF], F32, name=f"back{h}{u}", tag=f"yb{2 * u + h}")
                nc.tensor.transpose(back[h, u][:, t % 2, P * (k % 2) : P * (k % 2 + 1)], turned[:, P * k : P * (k + 1)], ident[:])

        score_a(0)
        score_a(1)
        score_b(0)
        score_a(2)
        score_b(1)
        clip(0)
        score_a(3)
        score_b(2)
        turn(0)
        clip(1)
        score_b(3)
        clip(2)
        turn(1)
        clip(3)
        turn(2)
        turn(3)

        res = [new(f"res{h}", [P, PACK, HALF], F32) for h in range(2)]

        def fetch(u, lo, hi, tag):
            tile = new(f"high{u}_{lo}", [P, 2, hi - lo], F32, tag)
            for e in range(2):
                nc.vector.tensor_copy(tile[:, e, :], b_win[2 * u + e][:].indirect(entries(n5_t, lo, hi)))
            return tile

        def finish2(h, u, high, cols):
            nc.vector.scalar_tensor_tensor(res[h][:, 2 * u : 2 * u + 2, cols], back[h, u][:, :, cols], -1.0, high[:, :, cols], ALU.mult, ALU.max)

        def store(h, u):
            rows = slice(2 * u, 2 * u + 2)
            nc.sync.dma_start(out_rows[:, rows, h * HALF : (h + 1) * HALF], res[h][:, rows, :])

        def quant2(lo, hi, resi):
            nc.vector.quantize_mx(out=ow[:, lo:hi].bitcast(FP8X4), scales=osc[:, lo:hi], in_=resi[:])

        def round2(name, src, width, copy):
            resi = new(name, [P, PACK * width], BF16)
            interleave(copy, resi, src)
            return resi

        whole = slice(0, HALF)
        high0 = fetch(0, 0, S, "gap2")
        finish2(0, 0, high0[:, :, :HALF], whole)
        store(0, 0)
        high01 = fetch(1, 0, HALF, "over2")
        finish2(1, 0, high0[:, :, HALF:], whole)
        store(1, 0)
        finish2(0, 1, high01, whole)
        store(0, 1)
        r0 = round2("r0", res[0][:], HALF, nc.scalar.copy)
        high11 = fetch(1, HALF, S, "over2")
        quant2(0, HALF, r0)
        nc.sync.dma_start(out_words[:, :HALF], ow[:, :HALF].bitcast(I32))
        finish2(1, 1, high11, slice(0, P))
        r1 = round2("r1", res[1][:, :, :P], P, nc.scalar.copy)
        finish2(1, 1, high11, slice(P, HALF))
        store(1, 1)
        r2 = round2("r2", res[1][:, :, P:], P, nc.vector.tensor_copy)
        quant2(HALF, HALF + P, r1)
        quant2(HALF + P, S, r2)
        nc.sync.dma_start(out_words[:, HALF:], ow[:, HALF:].bitcast(I32))
        for q in range(4):
            queue = nc.sync if q % 2 else nc.scalar
            queue.dma_start(out_2[0, 4 * q : 4 * q + 4, :].bitcast(I32), osc[32 * q : 32 * q + 4, :].bitcast(I32))
